import numpy as np
import ml_dtypes


def mxq(x, axis, fmt="e4m3"):
    dtype, down = {"e4m3": (ml_dtypes.float8_e4m3fn, 7), "e5m2": (ml_dtypes.float8_e5m2, 14)}[fmt]
    v = np.moveaxis(np.asarray(x, np.float32).astype(ml_dtypes.bfloat16).astype(np.float64), axis, -1)
    blocks = v.reshape(v.shape[:-1] + (-1, 32))
    amax = np.abs(blocks).max(-1, keepdims=True)
    byte = np.maximum(np.where(amax > 0, np.frexp(amax)[1] - 1 + 127, 0) - down, 1)
    scale = np.exp2(byte - 127.0)
    codes = (blocks / scale).astype(np.float32).astype(dtype).astype(np.float64)
    return np.moveaxis((codes * scale).reshape(v.shape), -1, axis)


WIDE = False


def mx_kscale(k):
    if not WIDE:
        return np.ones(k)
    levels = np.array([10, -10, 5, -5, 0])
    if k % 512:
        return np.exp2(np.random.permutation(np.resize(levels, k // 32))).repeat(32)
    a = np.empty((k // 512, 16))
    for p in range(k // 512):
        a[p, :8] = np.random.permutation(np.resize(levels, 8))
        for g in range(8):
            far = levels[np.abs(levels - a[p, g]) >= 10]
            a[p, g + 8] = far[np.random.randint(len(far))]
    return np.exp2(a.ravel()).repeat(32)


def f64(x):
    return np.asarray(x).astype(np.float64)


def striped(idx):
    return np.tile(idx.reshape(-1, 16).T, (8, 1)).astype(np.uint16)


def unstriped(offs):
    return offs[:16].T.reshape(-1).astype(np.int64)


def striped8(idx):
    return np.concatenate([x.reshape(-1, 16).T for x in idx]).astype(np.uint16)


def runs(offs, k):
    lists = np.stack([offs[16 * r : 16 * r + 16].T.reshape(-1) for r in range(8)]).astype(np.int64)
    return lists[np.arange(k) % 512 // 64]


def pack_weight(w):
    k, n = w.shape
    w = f64(np.asarray(w, np.float32).astype(ml_dtypes.bfloat16)).reshape(k // 32, 32, n)
    amax = np.abs(w).max(1)
    byte = np.clip(np.where(amax > 0, np.frexp(amax)[1] - 1 + 127 - 7, 1), 1, 254)
    scaled = (w * np.exp2(127.0 - byte)[:, None, :]).reshape(k, n).astype(np.float32)
    words = np.ascontiguousarray(scaled.reshape(k // 512, 128, 4, n).transpose(0, 1, 3, 2)).astype(ml_dtypes.float8_e4m3fn).view(np.uint8)
    return words, np.ascontiguousarray(byte.astype(np.uint8).reshape(k // 512, 16, n))


def unpack_weight(words, scales):
    g, p, n, _ = words.shape
    vals = np.ascontiguousarray(words).view(ml_dtypes.float8_e4m3fn).astype(np.float64) * np.repeat(np.exp2(scales.astype(np.float64) - 127.0), 8, axis=1)[..., None]
    return vals.transpose(0, 1, 3, 2).reshape(g * 512, n)


def relu(v):
    return np.maximum(v, 0.0)

def planes(y):
    n, m = y.shape
    v = y.astype(np.float32).astype(ml_dtypes.bfloat16).astype(np.float64).reshape(n // 32, 32, m)
    top = np.abs(v).max(1)
    byte = np.clip(np.where(top > 0, np.frexp(top)[1] - 1 + 127 - 7, 1), 1, 254)
    codes = (v * np.exp2(127.0 - byte)[:, None, :]).reshape(n, m).astype(np.float32).astype(ml_dtypes.float8_e4m3fn).view(np.uint8)
    words = codes.reshape(n // 512, 128, 4, m).transpose(0, 1, 3, 2)
    return np.ascontiguousarray(words), np.ascontiguousarray(byte.astype(np.uint8).reshape(n // 512, 16, m))


K, T, S, V, N, U, H = 512, 2048, 512, 512, 512, 1024, 512
P = 2 ** 7


def setup_inputs():
    n = np.random.standard_normal
    s = mx_kscale(K)[:, None]
    u = mx_kscale(H)
    packed_xT = pack_weight(n((K, T)) * s)
    packed_w2 = pack_weight(n((H, N)) / np.sqrt(H) / u[:, None])
    return {
        "x_words": packed_xT[0],
        "x_scales": packed_xT[1],
        "w1": (n((K, H)) / np.sqrt(K) / s * u).astype(np.float32),
        "w2_words": packed_w2[0],
        "w2_scales": packed_w2[1],
        "g1": np.tile(np.random.uniform(0.2, 1.0, V), (P, 1)).astype(np.float32),
        "g2": np.tile(np.random.uniform(0.2, 1.0, V), (P, 1)).astype(np.float32),
        "offs": striped(np.random.permutation(T)[:S]),
        "slot": striped8(np.stack([np.random.permutation(U)[:S] for _ in range(8)])),
        "c1": striped8(np.stack([np.random.permutation(U)[:V] for _ in range(8)])),
        "c2": striped8(np.stack([np.random.permutation(U)[:V] for _ in range(8)])),
    }


def reference(x_words, x_scales, w1, w2_words, w2_scales, g1, g2, offs, slot, c1, c2):
    xq = unpack_weight(x_words, x_scales)[:, unstriped(offs)]
    y = mxq(f64(w1), 0, "e4m3").T @ xq
    d = np.zeros((H, U))
    d[np.arange(H)[:, None], runs(slot, H)] = y
    z = relu(d)
    h = unpack_weight(w2_words, w2_scales).T @ mxq(z, 0, "e4m3")
    out_0 = (h[np.arange(N)[:, None], runs(c1, N)]) * f64(g1)[:1] + (h[np.arange(N)[:, None], runs(c2, N)]) * f64(g2)[:1]
    return (out_0,) + planes(out_0)

@@ -1,0 +1,201 @@
+from contextlib import ExitStack
+
+import concourse.mybir as mybir
+
+K, T, S, V, N, U, H = 512, 2048, 512, 512, 512, 1024, 512
+FLOPS = 2 * K * H * S + 2 * H * N * U
+
+F32 = mybir.dt.float32
+BF16 = mybir.dt.bfloat16
+I32 = mybir.dt.int32
+U32 = mybir.dt.uint32
+U16 = mybir.dt.uint16
+U8 = mybir.dt.uint8
+FP8X4 = mybir.dt.float8_e4m3fn_x4
+MULT = mybir.AluOpType.mult
+ADD = mybir.AluOpType.add
+RELU = mybir.ActivationFunctionType.Relu
+COPY = mybir.ActivationFunctionType.Copy
+
+P = 128
+PACK = 4
+PER_COLUMN = 16
+CHUNK = 256
+VA = 384
+
+
+def tile_picked_dcomb_relu_po_kernel(tc, x_words, x_scales, w1, w2_words, w2_scales, g1, g2, offs, slot, c1, c2, out_0, out_1, out_2):
+    nc = tc.nc
+    with ExitStack() as ctx:
+        keep = ctx.enter_context(tc.tile_pool(name="keep", bufs=1))
+        psum = ctx.enter_context(tc.psum_pool(name="psum", bufs=8))
+
+        def sb(name, shape, dtype):
+            return keep.tile(shape, dtype, name=name, align_bytes=64)
+
+        def bank(name, width):
+            return psum.tile([P, width], F32, name=name, tag="bank")
+
+        def scale_rows(queue, tile, rows):
+            for q in range(4):
+                queue.dma_start(out=tile[32 * q : 32 * q + 4, :].bitcast(I32), in_=rows[4 * q : 4 * q + 4, :].bitcast(I32))
+
+        offs_t = sb("offs_t", [P, S // PER_COLUMN], U16)
+        slot_t = sb("slot_t", [P, S // PER_COLUMN], U16)
+        c1_t = sb("c1_t", [P, V // PER_COLUMN], U16)
+        c2_t = sb("c2_t", [P, V // PER_COLUMN], U16)
+        xw = sb("xw", [P, T], U32)
+        xs = sb("xs", [P, T], U8)
+        w2w = sb("w2w", [P, N], U32)
+        w2s = sb("w2s", [P, N], U8)
+        w1_half = [sb("w1_half%d" % u, [P, PACK, H // 2], F32) for u in range(2)]
+        g_t = [sb("g%d" % u, [P, V], F32) for u in range(2)]
+        d = [sb("d%d" % t, [P, U], F32) for t in range(PACK)]
+
+        nc.vector.memset(xs[:].bitcast(I32), 0)
+        nc.sync.dma_start(offs_t[:], offs)
+        scale_rows(nc.scalar, xs, x_scales[0])
+        w1_rows = w1.rearrange("(p j) c -> p j c", j=PACK)
+        for u in range(2):
+            nc.sync.dma_start(out=w1_half[u][:], in_=w1_rows[:, :, u * H // 2 : (u + 1) * H // 2])
+        nc.sync.dma_start(out=xw[:].bitcast(I32), in_=x_words[0].rearrange("p n t -> p (n t)").bitcast(I32))
+        nc.vector.memset(w2s[:].bitcast(I32), 0)
+        scale_rows(nc.sync, w2s, w2_scales[0])
+        nc.sync.dma_start(slot_t[:], slot)
+        nc.sync.dma_start(out=w2w[:].bitcast(I32), in_=w2_words[0].rearrange("p n t -> p (n t)").bitcast(I32))
+        nc.sync.dma_start(c1_t[:], c1)
+        nc.sync.dma_start(c2_t[:], c2)
+        nc.sync.dma_start(out=g_t[0][:], in_=g1)
+        nc.sync.dma_start(out=g_t[1][:], in_=g2)
+        for t in range(PACK):
+            nc.vector.memset(d[t][:], 0.0)
+
+        xsg = sb("xsg", [P, S], U8)
+        nc.vector.tensor_copy(xsg[:], xs[:].indirect(offs_t[:]))
+
+        w1b = sb("w1b", [P, PACK, P, PACK], BF16)
+        for u in range(2):
+            dst = w1b[:, :, u * P // 2 : (u + 1) * P // 2, :].rearrange("p t m j -> p m t j")
+            src = w1_half[u][:].rearrange("p j (m t) -> p m t j", t=PACK)
+            if u == 0:
+                nc.scalar.activation(dst, src, COPY)
+            else:
+                nc.vector.tensor_copy(dst, src)
+        w1c = sb("w1c", [P, H], U32)
+        w1s = sb("w1s", [P, H], U8)
+        nc.vector.quantize_mx(out=w1c[:].bitcast(FP8X4), scales=w1s[:], in_=w1b[:].rearrange("p t m j -> p (t m j)"))
+
+        w2sd = sb("w2sd", [P, N], U8)
+        nc.vector.tensor_copy(w2sd[:].rearrange("p (t m) -> p m t", t=PACK), w2s[:].rearrange("p (m t) -> p m t", t=PACK))
+
+        xg = sb("xg", [P, S], U32)
+        for u in range(2):
+            nc.vector.tensor_copy(xg[:, u * 256 : (u + 1) * 256], xw[:].indirect(offs_t[:, u * 16 : (u + 1) * 16]))
+
+        w2d = sb("w2d", [P, N], U32)
+        nc.vector.tensor_copy(w2d[:].rearrange("p (t m) -> p m t", t=PACK), w2w[:].rearrange("p (m t) -> p m t", t=PACK))
+
+        def product(name, codes, scales, t, rhs, rhs_scales, cols):
+            acc = bank(name, cols.stop - cols.start)
+            nc.tensor.matmul_mx(
+                out=acc[:],
+                lhsT=codes[:, t * P : (t + 1) * P].bitcast(FP8X4),
+                lhsT_scale=scales[:, t * P : (t + 1) * P],
+                rhs=rhs[:, cols].bitcast(FP8X4),
+                rhs_scale=rhs_scales[:, cols],
+                start=True,
+                stop=True,
+            )
+            return acc
+
+        y = [sb("y%d" % t, [P, S], F32) for t in range(PACK)]
+        pieces = [(0, slice(0, 256)), (0, slice(256, 512))] + [(t, slice(0, S)) for t in range(1, PACK)]
+        for t, cols in pieces:
+            acc = product("y_acc", w1c, w1s, t, xg, xsg, cols)
+            nc.scalar.copy(y[t][:, cols], acc[:])
+
+        n_chunks = U // CHUNK
+        z = [sb("z%d" % c, [P, CHUNK, PACK], BF16) for c in range(n_chunks)]
+        for t, cols in pieces:
+            nc.vector.tensor_copy(d[t][:].indirect(slot_t[:, cols.start // PER_COLUMN : cols.stop // PER_COLUMN]), y[t][:, cols])
+            if cols.stop < S or t == PACK - 1:
+                continue
+            for c in range(n_chunks):
+                src = d[t][:, c * CHUNK : (c + 1) * CHUNK]
+                if t == 2 and c < 2:
+                    nc.scalar.activation(z[c][:, :, 2:4], src.unsqueeze(2).to_broadcast([P, CHUNK, 2]), RELU)
+                else:
+                    nc.scalar.activation(z[c][:, :, t], src, RELU)
+        for c in range(n_chunks):
+            src = d[3][:, c * CHUNK : (c + 1) * CHUNK]
+            if c < 2:
+                nc.vector.tensor_scalar_max(z[c][:, :, 3], src, 0.0)
+            else:
+                nc.scalar.activation(z[c][:, :, 3], src, RELU)
+
+        zc = sb("zc", [P, U], U32)
+        zs = sb("zs", [P, U], U8)
+        h = [sb("h%d" % t, [P, U], F32) for t in range(PACK)]
+        for c in (0, 2, 1, 3):
+            cols = slice(c * CHUNK, (c + 1) * CHUNK)
+            nc.vector.quantize_mx(out=zc[:, cols].bitcast(FP8X4), scales=zs[:, cols], in_=z[c][:].rearrange("p n t -> p (n t)"))
+            acc = product("h_acc", w2d, w2sd, 0, zc, zs, cols)
+            nc.scalar.copy(h[0][:, cols], acc[:])
+        for t in range(1, PACK):
+            for u in range(2):
+                cols = slice(u * 512, (u + 1) * 512)
+                acc = product("h_acc", w2d, w2sd, t, zc, zs, cols)
+                nc.scalar.copy(h[t][:, cols], acc[:])
+
+        out_rows = out_0.rearrange("(p t) v -> p t v", t=PACK)
+        oc = sb("oc", [P, V], U32)
+        os_ = sb("os", [P, V], U8)
+        words = out_1[0].rearrange("p n t -> p (n t)").bitcast(I32)
+        VB = V - VA
+        ra = [sb("ra%d" % u, [P, PACK, VA], F32) for u in range(2)]
+        rb = [sb("rb%d" % u, [P, PACK, VB], F32) for u in range(2)]
+        oa = sb("oa", [P, PACK, VA], F32)
+        ob = sb("ob", [P, PACK, VB], F32)
+        oa16 = sb("oa16", [P, VA, PACK], BF16)
+        ob16 = sb("ob16", [P, VB, PACK], BF16)
+        lists = (c1_t, c2_t)
+
+        def read(dst, u, t, cols):
+            nc.vector.tensor_tensor(dst[u][:, t, :], h[t][:].indirect(lists[u][:, cols.start // PER_COLUMN : cols.stop // PER_COLUMN]), g_t[u][:, cols], MULT)
+
+        def add_a(t):
+            nc.vector.tensor_tensor(oa[:, t, :], ra[0][:, t, :], ra[1][:, t, :], ADD)
+            nc.sync.dma_start(out=out_rows[:, t, 0:VA], in_=oa[:, t, :])
+
+        def quant(src, cols):
+            nc.vector.quantize_mx(out=oc[:, cols].bitcast(FP8X4), scales=os_[:, cols], in_=src.rearrange("p n t -> p (n t)"))
+
+        ca, cb = slice(0, VA), slice(VA, V)
+        for t in range(PACK):
+            read(ra, 0, t, ca)
+            if t > 0:
+                add_a(t - 1)
+            read(ra, 1, t, ca)
+        read(rb, 0, 0, cb)
+        add_a(3)
+        parts = (slice(0, 256), slice(256, VA))
+        for cols in parts:
+            nc.scalar.copy(oa16[:, cols, :], oa[:, :, cols].rearrange("p t n -> p n t"))
+        read(rb, 1, 0, cb)
+        for t in (1, 2):
+            read(rb, 0, t, cb)
+            read(rb, 1, t, cb)
+        read(rb, 0, 3, cb)
+        nc.vector.tensor_tensor(ob[:, 0:3, :], rb[0][:, 0:3, :], rb[1][:, 0:3, :], ADD)
+        read(rb, 1, 3, cb)
+        quant(oa16[:, parts[0], :], parts[0])
+        nc.vector.tensor_tensor(ob[:, 3, :], rb[0][:, 3, :], rb[1][:, 3, :], ADD)
+        nc.sync.dma_start(out=out_rows[:, :, cb], in_=ob[:])
+        quant(oa16[:, parts[1], :], parts[1])
+        nc.scalar.dma_start(out=words[:, ca], in_=oc[:, ca].bitcast(I32))
+        nc.vector.tensor_copy(ob16[:], ob[:].rearrange("p t n -> p n t"))
+        quant(ob16[:], cb)
+        nc.sync.dma_start(out=words[:, cb], in_=oc[:, cb].bitcast(I32))
+        for q in range(4):
+            queue = nc.scalar if q % 2 == 0 else nc.sync
+            queue.dma_start(out=out_2[0, 4 * q : 4 * q + 4, :].bitcast(I32), in_=os_[32 * q : 32 * q + 4, :].bitcast(I32))

@@ -1,6 +1,7 @@
 from contextlib import ExitStack
 
 import concourse.mybir as mybir
+from concourse.masks import make_identity
 
 K, T, S, V, N, U, H = 512, 2048, 512, 512, 512, 1024, 512
 FLOPS = 2 * K * H * S + 2 * H * N * U
@@ -22,13 +23,16 @@ PACK = 4
 PER_COLUMN = 16
 CHUNK = 256
 VA = 384
+ORDER = (2, 0, 1, 3)
+SPLIT = 640
 
 
 def tile_picked_dcomb_relu_po_kernel(tc, x_words, x_scales, w1, w2_words, w2_scales, g1, g2, offs, slot, c1, c2, out_0, out_1, out_2):
     nc = tc.nc
     with ExitStack() as ctx:
         keep = ctx.enter_context(tc.tile_pool(name="keep", bufs=1))
-        psum = ctx.enter_context(tc.psum_pool(name="psum", bufs=8))
+        psum = ctx.enter_context(tc.psum_pool(name="psum", bufs=6))
+        turns = ctx.enter_context(tc.psum_pool(name="turns", bufs=2))
 
         def sb(name, shape, dtype):
             return keep.tile(shape, dtype, name=name, align_bytes=64)
@@ -50,25 +54,30 @@ def tile_picked_dcomb_relu_po_kernel(tc, x_words, x_scales, w1, w2_words, w2_sca
         w2s = sb("w2s", [P, N], U8)
         w1_half = [sb("w1_half%d" % u, [P, PACK, H // 2], F32) for u in range(2)]
         g_t = [sb("g%d" % u, [P, V], F32) for u in range(2)]
-        d = [sb("d%d" % t, [P, U], F32) for t in range(PACK)]
+        d = [keep.tile([P, U], F32, name="d%d" % t, tag="d%d" % t, align_bytes=64) for t in range(PACK)]
 
-        nc.vector.memset(xs[:].bitcast(I32), 0)
-        nc.sync.dma_start(offs_t[:], offs)
-        scale_rows(nc.scalar, xs, x_scales[0])
+        nc.gpsimd.memset(xs[:].bitcast(I32), 0)
         w1_rows = w1.rearrange("(p j) c -> p j c", j=PACK)
-        for u in range(2):
-            nc.sync.dma_start(out=w1_half[u][:], in_=w1_rows[:, :, u * H // 2 : (u + 1) * H // 2])
+        nc.sync.dma_start(out=w1_half[0][:], in_=w1_rows[:, :, 0 : H // 2])
+        nc.sync.dma_start(offs_t[:], offs)
+        scale_rows(nc.sync, xs, x_scales[0])
+        nc.sync.dma_start(out=w1_half[1][:], in_=w1_rows[:, :, H // 2 : H])
         nc.sync.dma_start(out=xw[:].bitcast(I32), in_=x_words[0].rearrange("p n t -> p (n t)").bitcast(I32))
-        nc.vector.memset(w2s[:].bitcast(I32), 0)
-        scale_rows(nc.sync, w2s, w2_scales[0])
         nc.sync.dma_start(slot_t[:], slot)
+        nc.vector.memset(w2s[:].bitcast(I32), 0)
         nc.sync.dma_start(out=w2w[:].bitcast(I32), in_=w2_words[0].rearrange("p n t -> p (n t)").bitcast(I32))
+        scale_rows(nc.sync, w2s, w2_scales[0])
         nc.sync.dma_start(c1_t[:], c1)
         nc.sync.dma_start(c2_t[:], c2)
         nc.sync.dma_start(out=g_t[0][:], in_=g1)
         nc.sync.dma_start(out=g_t[1][:], in_=g2)
-        for t in range(PACK):
+        for t in ORDER[:2]:
             nc.vector.memset(d[t][:], 0.0)
+        for t in ORDER[2:]:
+            nc.gpsimd.memset(d[t][:], 0.0)
+
+        ident = sb("ident", [P, P], F32)
+        make_identity(nc, ident[:])
 
         xsg = sb("xsg", [P, S], U8)
         nc.vector.tensor_copy(xsg[:], xs[:].indirect(offs_t[:]))
@@ -85,22 +94,16 @@ def tile_picked_dcomb_relu_po_kernel(tc, x_words, x_scales, w1, w2_words, w2_sca
         w1s = sb("w1s", [P, H], U8)
         nc.vector.quantize_mx(out=w1c[:].bitcast(FP8X4), scales=w1s[:], in_=w1b[:].rearrange("p t m j -> p (t m j)"))
 
-        w2sd = sb("w2sd", [P, N], U8)
-        nc.vector.tensor_copy(w2sd[:].rearrange("p (t m) -> p m t", t=PACK), w2s[:].rearrange("p (m t) -> p m t", t=PACK))
-
         xg = sb("xg", [P, S], U32)
         for u in range(2):
             nc.vector.tensor_copy(xg[:, u * 256 : (u + 1) * 256], xw[:].indirect(offs_t[:, u * 16 : (u + 1) * 16]))
 
-        w2d = sb("w2d", [P, N], U32)
-        nc.vector.tensor_copy(w2d[:].rearrange("p (t m) -> p m t", t=PACK), w2w[:].rearrange("p (m t) -> p m t", t=PACK))
-
-        def product(name, codes, scales, t, rhs, rhs_scales, cols):
+        def product(name, codes, scales, rhs, rhs_scales, cols):
             acc = bank(name, cols.stop - cols.start)
             nc.tensor.matmul_mx(
                 out=acc[:],
-                lhsT=codes[:, t * P : (t + 1) * P].bitcast(FP8X4),
-                lhsT_scale=scales[:, t * P : (t + 1) * P],
+                lhsT=codes.bitcast(FP8X4),
+                lhsT_scale=scales,
                 rhs=rhs[:, cols].bitcast(FP8X4),
                 rhs_scale=rhs_scales[:, cols],
                 start=True,
@@ -108,43 +111,67 @@ def tile_picked_dcomb_relu_po_kernel(tc, x_words, x_scales, w1, w2_words, w2_sca
             )
             return acc
 
-        y = [sb("y%d" % t, [P, S], F32) for t in range(PACK)]
-        pieces = [(0, slice(0, 256)), (0, slice(256, 512))] + [(t, slice(0, S)) for t in range(1, PACK)]
-        for t, cols in pieces:
-            acc = product("y_acc", w1c, w1s, t, xg, xsg, cols)
+        first, last = ORDER[0], ORDER[-1]
+        y = {t: keep.tile([P, S], F32, name="y%d" % t, tag="y%d" % t, align_bytes=64) for t in ORDER[1:-1]}
+        y[first] = keep.tile([P, S], F32, name="y_first", tag="y_ends", align_bytes=64)
+        halves = (slice(0, S // 2), slice(S // 2, S))
+        for t, cols in [(first, half) for half in halves] + [(t, slice(0, S)) for t in ORDER[1:-1]]:
+            acc = product("y_acc", w1c[:, t * P : (t + 1) * P], w1s[:, t * P : (t + 1) * P], xg, xsg, cols)
             nc.scalar.copy(y[t][:, cols], acc[:])
+        last_acc = product("y_acc", w1c[:, last * P : (last + 1) * P], w1s[:, last * P : (last + 1) * P], xg, xsg, slice(0, S))
+
+        w2w_mt = w2w[:].rearrange("p (m t) -> p m t", t=PACK)
+        w2s_mt = w2s[:].rearrange("p (m t) -> p m t", t=PACK)
 
         n_chunks = U // CHUNK
-        z = [sb("z%d" % c, [P, CHUNK, PACK], BF16) for c in range(n_chunks)]
-        for t, cols in pieces:
+        z = [keep.tile([P, CHUNK, PACK], BF16, name="z%d" % c, tag="z%d" % c, align_bytes=64) for c in range(n_chunks)]
+
+        def scatter(t, cols):
             nc.vector.tensor_copy(d[t][:].indirect(slot_t[:, cols.start // PER_COLUMN : cols.stop // PER_COLUMN]), y[t][:, cols])
-            if cols.stop < S or t == PACK - 1:
-                continue
+
+        def round_plane(t, lo, hi, on_vector):
             for c in range(n_chunks):
-                src = d[t][:, c * CHUNK : (c + 1) * CHUNK]
-                if t == 2 and c < 2:
-                    nc.scalar.activation(z[c][:, :, 2:4], src.unsqueeze(2).to_broadcast([P, CHUNK, 2]), RELU)
-                else:
-                    nc.scalar.activation(z[c][:, :, t], src, RELU)
-        for c in range(n_chunks):
-            src = d[3][:, c * CHUNK : (c + 1) * CHUNK]
-            if c < 2:
-                nc.vector.tensor_scalar_max(z[c][:, :, 3], src, 0.0)
-            else:
-                nc.scalar.activation(z[c][:, :, 3], src, RELU)
+                a, b = max(lo, c * CHUNK), min(hi, (c + 1) * CHUNK)
+                if a < b:
+                    dst = z[c][:, a - c * CHUNK : b - c * CHUNK, t]
+                    if on_vector:
+                        nc.vector.tensor_scalar_max(dst, d[t][:, a:b], 0.0)
+                    else:
+                        nc.scalar.activation(dst, d[t][:, a:b], RELU)
+
+        scatter(first, halves[0])
+        w2w_0 = sb("w2w_0", [P, P], U32)
+        nc.vector.tensor_copy(w2w_0[:], w2w_mt[:, :, 0])
+        w2s_0 = sb("w2s_0", [P, P], U8)
+        nc.vector.tensor_copy(w2s_0[:], w2s_mt[:, :, 0])
+        scatter(first, halves[1])
+        round_plane(first, 0, U, False)
+        y[last] = keep.tile([P, S], F32, name="y_last", tag="y_ends", align_bytes=64)
+        nc.scalar.copy(y[last][:], last_acc[:])
+        for t in ORDER[1:-1]:
+            scatter(t, slice(0, S))
+            round_plane(t, 0, U, False)
+        scatter(last, slice(0, S))
+        round_plane(last, SPLIT, U, False)
+        round_plane(last, 0, SPLIT, True)
 
         zc = sb("zc", [P, U], U32)
         zs = sb("zs", [P, U], U8)
         h = [sb("h%d" % t, [P, U], F32) for t in range(PACK)]
-        for c in (0, 2, 1, 3):
-            cols = slice(c * CHUNK, (c + 1) * CHUNK)
-            nc.vector.quantize_mx(out=zc[:, cols].bitcast(FP8X4), scales=zs[:, cols], in_=z[c][:].rearrange("p n t -> p (n t)"))
-            acc = product("h_acc", w2d, w2sd, 0, zc, zs, cols)
+        for lo, hi in ((0, 256), (256, 512), (512, 768), (768, 896), (896, 1024)):
+            c = lo // CHUNK
+            cols = slice(lo, hi)
+            nc.vector.quantize_mx(out=zc[:, cols].bitcast(FP8X4), scales=zs[:, cols], in_=z[c][:, lo - c * CHUNK : hi - c * CHUNK, :].rearrange("p n t -> p (n t)"))
+            acc = product("h_acc", w2w_0[:], w2s_0[:], zc, zs, cols)
             nc.scalar.copy(h[0][:, cols], acc[:])
+        w2w_r = keep.tile([P, PACK - 1, P], U32, name="w2w_r", tag="z3", align_bytes=64)
+        w2s_r = keep.tile([P, PACK - 1, P], U8, name="w2s_r", tag="z2", align_bytes=64)
+        nc.vector.tensor_copy(w2w_r[:].rearrange("p t m -> p m t"), w2w_mt[:, :, 1:])
+        nc.vector.tensor_copy(w2s_r[:].rearrange("p t m -> p m t"), w2s_mt[:, :, 1:])
         for t in range(1, PACK):
             for u in range(2):
                 cols = slice(u * 512, (u + 1) * 512)
-                acc = product("h_acc", w2d, w2sd, t, zc, zs, cols)
+                acc = product("h_acc", w2w_r[:, t - 1, :], w2s_r[:, t - 1, :], zc, zs, cols)
                 nc.scalar.copy(h[t][:, cols], acc[:])
 
         out_rows = out_0.rearrange("(p t) v -> p t v", t=PACK)
@@ -153,7 +180,6 @@ def tile_picked_dcomb_relu_po_kernel(tc, x_words, x_scales, w1, w2_words, w2_sca
         words = out_1[0].rearrange("p n t -> p (n t)").bitcast(I32)
         VB = V - VA
         ra = [sb("ra%d" % u, [P, PACK, VA], F32) for u in range(2)]
-        rb = [sb("rb%d" % u, [P, PACK, VB], F32) for u in range(2)]
         oa = sb("oa", [P, PACK, VA], F32)
         ob = sb("ob", [P, PACK, VB], F32)
         oa16 = sb("oa16", [P, VA, PACK], BF16)
@@ -167,15 +193,38 @@ def tile_picked_dcomb_relu_po_kernel(tc, x_words, x_scales, w1, w2_words, w2_sca
             nc.vector.tensor_tensor(oa[:, t, :], ra[0][:, t, :], ra[1][:, t, :], ADD)
             nc.sync.dma_start(out=out_rows[:, t, 0:VA], in_=oa[:, t, :])
 
+        blocks = [slice(b, b + P) for b in range(0, VA, P)]
+        staged = [keep.tile([P, VA], F32, name="staged%d" % t, tag="staged%d" % t, align_bytes=64) for t in range(2)]
+
+        def add_turned(t):
+            turned = turns.tile([P, VA], F32, name="turned", tag="turn")
+            for cols in blocks:
+                for u in range(2):
+                    nc.tensor.matmul(turned[:, cols], ra[u][:, t, cols], ident[:], start=(u == 0), stop=(u == 1), is_transpose=True)
+            nc.scalar.copy(staged[t][:], turned[:])
+
+        def turn_back(t):
+            back = turns.tile([P, VA], F32, name="back", tag="turn")
+            for cols in blocks:
+                nc.tensor.transpose(back[:, cols], staged[t][:, cols], ident[:])
+            nc.scalar.copy(oa[:, t, :], back[:])
+            nc.sync.dma_start(out=out_rows[:, t, 0:VA], in_=oa[:, t, :])
+
         def quant(src, cols):
             nc.vector.quantize_mx(out=oc[:, cols].bitcast(FP8X4), scales=os_[:, cols], in_=src.rearrange("p n t -> p (n t)"))
 
         ca, cb = slice(0, VA), slice(VA, V)
         for t in range(PACK):
             read(ra, 0, t, ca)
-            if t > 0:
-                add_a(t - 1)
+            if t == 3:
+                add_a(2)
             read(ra, 1, t, ca)
+            if t < 2:
+                add_turned(t)
+            if t == 1:
+                turn_back(0)
+                turn_back(1)
+        rb = [keep.tile([P, PACK, VB], F32, name="rb%d" % u, tag="staged%d" % u, align_bytes=64) for u in range(2)]
         read(rb, 0, 0, cb)
         add_a(3)
         parts = (slice(0, 256), slice(256, VA))

@@ -19,61 +19,90 @@ RELU = mybir.ActivationFunctionType.Relu
 COPY = mybir.ActivationFunctionType.Copy
 
 P = 128
-PACK = 4
-PER_COLUMN = 16
-CHUNK = 256
-VA = 384
-ORDER = (2, 0, 1, 3)
-SPLIT = 640
+PLANES = 4
+ENTRIES_PER_COLUMN = 16
+QUADRANT = 32
+SCALE_ROWS = 16
+BANK = 512
+PRODUCT_BANKS = 6
+TURN_BANKS = 2
+
+SCATTER_ORDER = (2, 0, 1, 3)
+Z_CHUNK = 256
+VECTOR_PLACES = 640
+H0_PIECES = ((0, 256), (256, 512), (512, 768), (768, 896), (896, 1024))
+EARLY = 384
+LATE = V - EARLY
+TURNED_PLANES = 2
 
 
 def tile_picked_dcomb_relu_po_kernel(tc, x_words, x_scales, w1, w2_words, w2_scales, g1, g2, offs, slot, c1, c2, out_0, out_1, out_2):
     nc = tc.nc
     with ExitStack() as ctx:
         keep = ctx.enter_context(tc.tile_pool(name="keep", bufs=1))
-        psum = ctx.enter_context(tc.psum_pool(name="psum", bufs=6))
-        turns = ctx.enter_context(tc.psum_pool(name="turns", bufs=2))
+        psum = ctx.enter_context(tc.psum_pool(name="psum", bufs=PRODUCT_BANKS))
+        turns = ctx.enter_context(tc.psum_pool(name="turns", bufs=TURN_BANKS))
 
-        def sb(name, shape, dtype):
-            return keep.tile(shape, dtype, name=name, align_bytes=64)
+        def sb(name, shape, dtype, buffer=None):
+            return keep.tile(shape, dtype, name=name, tag=buffer or name, align_bytes=64)
 
-        def bank(name, width):
-            return psum.tile([P, width], F32, name=name, tag="bank")
+        def entries(offsets, cols):
+            return offsets[:, cols.start // ENTRIES_PER_COLUMN : cols.stop // ENTRIES_PER_COLUMN]
 
-        def scale_rows(queue, tile, rows):
-            for q in range(4):
-                queue.dma_start(out=tile[32 * q : 32 * q + 4, :].bitcast(I32), in_=rows[4 * q : 4 * q + 4, :].bitcast(I32))
+        def as_words(packed):
+            return packed[0].rearrange("p n t -> p (n t)").bitcast(I32)
 
-        offs_t = sb("offs_t", [P, S // PER_COLUMN], U16)
-        slot_t = sb("slot_t", [P, S // PER_COLUMN], U16)
-        c1_t = sb("c1_t", [P, V // PER_COLUMN], U16)
-        c2_t = sb("c2_t", [P, V // PER_COLUMN], U16)
+        def load_scale_rows(tile, rows):
+            for r in range(4):
+                nc.sync.dma_start(out=tile[r:P:QUADRANT, :].bitcast(I32), in_=rows[r:SCALE_ROWS:4, :].bitcast(I32))
+
+        def product(name, codes, scales, moving, moving_scales, cols):
+            acc = psum.tile([P, cols.stop - cols.start], F32, name=name, tag="bank")
+            nc.tensor.matmul_mx(
+                out=acc[:],
+                lhsT=codes.bitcast(FP8X4),
+                lhsT_scale=scales,
+                rhs=moving[:, cols].bitcast(FP8X4),
+                rhs_scale=moving_scales[:, cols],
+                start=True,
+                stop=True,
+            )
+            return acc
+
+        def quantise(codes, scales, cols, grouped):
+            nc.vector.quantize_mx(out=codes[:, cols].bitcast(FP8X4), scales=scales[:, cols], in_=grouped.rearrange("p n t -> p (n t)"))
+
+        offs_t = sb("offs_t", [P, S // ENTRIES_PER_COLUMN], U16)
+        slot_t = sb("slot_t", [P, S // ENTRIES_PER_COLUMN], U16)
+        c1_t = sb("c1_t", [P, V // ENTRIES_PER_COLUMN], U16)
+        c2_t = sb("c2_t", [P, V // ENTRIES_PER_COLUMN], U16)
         xw = sb("xw", [P, T], U32)
         xs = sb("xs", [P, T], U8)
         w2w = sb("w2w", [P, N], U32)
         w2s = sb("w2s", [P, N], U8)
-        w1_half = [sb("w1_half%d" % u, [P, PACK, H // 2], F32) for u in range(2)]
+        w1_half = [sb("w1_half%d" % u, [P, PLANES, H // 2], F32) for u in range(2)]
         g_t = [sb("g%d" % u, [P, V], F32) for u in range(2)]
-        d = [keep.tile([P, U], F32, name="d%d" % t, tag="d%d" % t, align_bytes=64) for t in range(PACK)]
+        d = [sb("d%d" % t, [P, U], F32) for t in range(PLANES)]
 
         nc.gpsimd.memset(xs[:].bitcast(I32), 0)
-        w1_rows = w1.rearrange("(p j) c -> p j c", j=PACK)
+        w1_rows = w1.rearrange("(p j) c -> p j c", j=PLANES)
         nc.sync.dma_start(out=w1_half[0][:], in_=w1_rows[:, :, 0 : H // 2])
         nc.sync.dma_start(offs_t[:], offs)
-        scale_rows(nc.sync, xs, x_scales[0])
+        load_scale_rows(xs, x_scales[0])
         nc.sync.dma_start(out=w1_half[1][:], in_=w1_rows[:, :, H // 2 : H])
-        nc.sync.dma_start(out=xw[:].bitcast(I32), in_=x_words[0].rearrange("p n t -> p (n t)").bitcast(I32))
+        nc.sync.dma_start(out=xw[:].bitcast(I32), in_=as_words(x_words))
         nc.sync.dma_start(slot_t[:], slot)
         nc.vector.memset(w2s[:].bitcast(I32), 0)
-        nc.sync.dma_start(out=w2w[:].bitcast(I32), in_=w2_words[0].rearrange("p n t -> p (n t)").bitcast(I32))
-        scale_rows(nc.sync, w2s, w2_scales[0])
+        nc.sync.dma_start(out=w2w[:].bitcast(I32), in_=as_words(w2_words))
+        load_scale_rows(w2s, w2_scales[0])
         nc.sync.dma_start(c1_t[:], c1)
         nc.sync.dma_start(c2_t[:], c2)
         nc.sync.dma_start(out=g_t[0][:], in_=g1)
         nc.sync.dma_start(out=g_t[1][:], in_=g2)
-        for t in ORDER[:2]:
+
+        for t in SCATTER_ORDER[:2]:
             nc.vector.memset(d[t][:], 0.0)
-        for t in ORDER[2:]:
+        for t in SCATTER_ORDER[2:]:
             nc.gpsimd.memset(d[t][:], 0.0)
 
         ident = sb("ident", [P, P], F32)
@@ -82,62 +111,51 @@ def tile_picked_dcomb_relu_po_kernel(tc, x_words, x_scales, w1, w2_words, w2_sca
         xsg = sb("xsg", [P, S], U8)
         nc.vector.tensor_copy(xsg[:], xs[:].indirect(offs_t[:]))
 
-        w1b = sb("w1b", [P, PACK, P, PACK], BF16)
-        for u in range(2):
-            dst = w1b[:, :, u * P // 2 : (u + 1) * P // 2, :].rearrange("p t m j -> p m t j")
-            src = w1_half[u][:].rearrange("p j (m t) -> p m t j", t=PACK)
-            if u == 0:
-                nc.scalar.activation(dst, src, COPY)
-            else:
-                nc.vector.tensor_copy(dst, src)
+        w1b = sb("w1b", [P, PLANES, P, PLANES], BF16)
+        w1_dst = [w1b[:, :, u * P // 2 : (u + 1) * P // 2, :].rearrange("p t m j -> p m t j") for u in range(2)]
+        w1_src = [w1_half[u][:].rearrange("p j (m t) -> p m t j", t=PLANES) for u in range(2)]
+        nc.scalar.activation(w1_dst[0], w1_src[0], COPY)
+        nc.vector.tensor_copy(w1_dst[1], w1_src[1])
         w1c = sb("w1c", [P, H], U32)
         w1s = sb("w1s", [P, H], U8)
-        nc.vector.quantize_mx(out=w1c[:].bitcast(FP8X4), scales=w1s[:], in_=w1b[:].rearrange("p t m j -> p (t m j)"))
+        quantise(w1c, w1s, slice(0, H), w1b[:].rearrange("p t m j -> p (t m) j"))
 
-        xg = sb("xg", [P, S], U32)
-        for u in range(2):
-            nc.vector.tensor_copy(xg[:, u * 256 : (u + 1) * 256], xw[:].indirect(offs_t[:, u * 16 : (u + 1) * 16]))
-
-        def product(name, codes, scales, rhs, rhs_scales, cols):
-            acc = bank(name, cols.stop - cols.start)
-            nc.tensor.matmul_mx(
-                out=acc[:],
-                lhsT=codes.bitcast(FP8X4),
-                lhsT_scale=scales,
-                rhs=rhs[:, cols].bitcast(FP8X4),
-                rhs_scale=rhs_scales[:, cols],
-                start=True,
-                stop=True,
-            )
-            return acc
-
-        first, last = ORDER[0], ORDER[-1]
-        y = {t: keep.tile([P, S], F32, name="y%d" % t, tag="y%d" % t, align_bytes=64) for t in ORDER[1:-1]}
-        y[first] = keep.tile([P, S], F32, name="y_first", tag="y_ends", align_bytes=64)
         halves = (slice(0, S // 2), slice(S // 2, S))
-        for t, cols in [(first, half) for half in halves] + [(t, slice(0, S)) for t in ORDER[1:-1]]:
-            acc = product("y_acc", w1c[:, t * P : (t + 1) * P], w1s[:, t * P : (t + 1) * P], xg, xsg, cols)
+        xg = sb("xg", [P, S], U32)
+        for cols in halves:
+            nc.vector.tensor_copy(xg[:, cols], xw[:].indirect(entries(offs_t, cols)))
+
+        def y_product(t, cols):
+            return product("y_acc", w1c[:, t * P : (t + 1) * P], w1s[:, t * P : (t + 1) * P], xg, xsg, cols)
+
+        first, middle, last = SCATTER_ORDER[0], SCATTER_ORDER[1:-1], SCATTER_ORDER[-1]
+        tokens = slice(0, S)
+        y = {t: sb("y%d" % t, [P, S], F32) for t in middle}
+        y[first] = sb("y_first", [P, S], F32, buffer="y_ends")
+        for t, cols in [(first, half) for half in halves] + [(t, tokens) for t in middle]:
+            acc = y_product(t, cols)
             nc.scalar.copy(y[t][:, cols], acc[:])
-        last_acc = product("y_acc", w1c[:, last * P : (last + 1) * P], w1s[:, last * P : (last + 1) * P], xg, xsg, slice(0, S))
+        last_acc = y_product(last, tokens)
 
-        w2w_mt = w2w[:].rearrange("p (m t) -> p m t", t=PACK)
-        w2s_mt = w2s[:].rearrange("p (m t) -> p m t", t=PACK)
+        w2w_mt = w2w[:].rearrange("p (m t) -> p m t", t=PLANES)
+        w2s_mt = w2s[:].rearrange("p (m t) -> p m t", t=PLANES)
 
-        n_chunks = U // CHUNK
-        z = [keep.tile([P, CHUNK, PACK], BF16, name="z%d" % c, tag="z%d" % c, align_bytes=64) for c in range(n_chunks)]
+        n_chunks = U // Z_CHUNK
+        z = [sb("z%d" % c, [P, Z_CHUNK, PLANES], BF16) for c in range(n_chunks)]
 
         def scatter(t, cols):
-            nc.vector.tensor_copy(d[t][:].indirect(slot_t[:, cols.start // PER_COLUMN : cols.stop // PER_COLUMN]), y[t][:, cols])
+            nc.vector.tensor_copy(d[t][:].indirect(entries(slot_t, cols)), y[t][:, cols])
 
-        def round_plane(t, lo, hi, on_vector):
-            for c in range(n_chunks):
-                a, b = max(lo, c * CHUNK), min(hi, (c + 1) * CHUNK)
-                if a < b:
-                    dst = z[c][:, a - c * CHUNK : b - c * CHUNK, t]
-                    if on_vector:
-                        nc.vector.tensor_scalar_max(dst, d[t][:, a:b], 0.0)
-                    else:
-                        nc.scalar.activation(dst, d[t][:, a:b], RELU)
+        def relu_on_scalar(dst, src):
+            nc.scalar.activation(dst, src, RELU)
+
+        def relu_on_vector(dst, src):
+            nc.vector.tensor_scalar_max(dst, src, 0.0)
+
+        def round_plane(t, lo, hi, relu):
+            for c in range(lo // Z_CHUNK, (hi - 1) // Z_CHUNK + 1):
+                a, b = max(lo, c * Z_CHUNK), min(hi, (c + 1) * Z_CHUNK)
+                relu(z[c][:, a - c * Z_CHUNK : b - c * Z_CHUNK, t], d[t][:, a:b])
 
         scatter(first, halves[0])
         w2w_0 = sb("w2w_0", [P, P], U32)
@@ -145,106 +163,112 @@ def tile_picked_dcomb_relu_po_kernel(tc, x_words, x_scales, w1, w2_words, w2_sca
         w2s_0 = sb("w2s_0", [P, P], U8)
         nc.vector.tensor_copy(w2s_0[:], w2s_mt[:, :, 0])
         scatter(first, halves[1])
-        round_plane(first, 0, U, False)
-        y[last] = keep.tile([P, S], F32, name="y_last", tag="y_ends", align_bytes=64)
+        round_plane(first, 0, U, relu_on_scalar)
+        y[last] = sb("y_last", [P, S], F32, buffer="y_ends")
         nc.scalar.copy(y[last][:], last_acc[:])
-        for t in ORDER[1:-1]:
-            scatter(t, slice(0, S))
-            round_plane(t, 0, U, False)
-        scatter(last, slice(0, S))
-        round_plane(last, SPLIT, U, False)
-        round_plane(last, 0, SPLIT, True)
+        for t in middle:
+            scatter(t, tokens)
+            round_plane(t, 0, U, relu_on_scalar)
+        scatter(last, tokens)
+        round_plane(last, VECTOR_PLACES, U, relu_on_scalar)
+        round_plane(last, 0, VECTOR_PLACES, relu_on_vector)
 
         zc = sb("zc", [P, U], U32)
         zs = sb("zs", [P, U], U8)
-        h = [sb("h%d" % t, [P, U], F32) for t in range(PACK)]
-        for lo, hi in ((0, 256), (256, 512), (512, 768), (768, 896), (896, 1024)):
-            c = lo // CHUNK
+        h = [sb("h%d" % t, [P, U], F32) for t in range(PLANES)]
+        for lo, hi in H0_PIECES:
+            c = lo // Z_CHUNK
             cols = slice(lo, hi)
-            nc.vector.quantize_mx(out=zc[:, cols].bitcast(FP8X4), scales=zs[:, cols], in_=z[c][:, lo - c * CHUNK : hi - c * CHUNK, :].rearrange("p n t -> p (n t)"))
+            quantise(zc, zs, cols, z[c][:, lo - c * Z_CHUNK : hi - c * Z_CHUNK, :])
             acc = product("h_acc", w2w_0[:], w2s_0[:], zc, zs, cols)
             nc.scalar.copy(h[0][:, cols], acc[:])
-        w2w_r = keep.tile([P, PACK - 1, P], U32, name="w2w_r", tag="z3", align_bytes=64)
-        w2s_r = keep.tile([P, PACK - 1, P], U8, name="w2s_r", tag="z2", align_bytes=64)
+
+        w2w_r = sb("w2w_r", [P, PLANES - 1, P], U32, buffer="z%d" % (n_chunks - 1))
+        w2s_r = sb("w2s_r", [P, PLANES - 1, P], U8, buffer="z%d" % (n_chunks - 2))
         nc.vector.tensor_copy(w2w_r[:].rearrange("p t m -> p m t"), w2w_mt[:, :, 1:])
         nc.vector.tensor_copy(w2s_r[:].rearrange("p t m -> p m t"), w2s_mt[:, :, 1:])
-        for t in range(1, PACK):
-            for u in range(2):
-                cols = slice(u * 512, (u + 1) * 512)
+        for t in range(1, PLANES):
+            for lo in range(0, U, BANK):
+                cols = slice(lo, lo + BANK)
                 acc = product("h_acc", w2w_r[:, t - 1, :], w2s_r[:, t - 1, :], zc, zs, cols)
                 nc.scalar.copy(h[t][:, cols], acc[:])
 
-        out_rows = out_0.rearrange("(p t) v -> p t v", t=PACK)
+        out_rows = out_0.rearrange("(p t) v -> p t v", t=PLANES)
         oc = sb("oc", [P, V], U32)
-        os_ = sb("os", [P, V], U8)
-        words = out_1[0].rearrange("p n t -> p (n t)").bitcast(I32)
-        VB = V - VA
-        ra = [sb("ra%d" % u, [P, PACK, VA], F32) for u in range(2)]
-        oa = sb("oa", [P, PACK, VA], F32)
-        ob = sb("ob", [P, PACK, VB], F32)
-        oa16 = sb("oa16", [P, VA, PACK], BF16)
-        ob16 = sb("ob16", [P, VB, PACK], BF16)
+        osc = sb("os", [P, V], U8)
+        out_words = as_words(out_1)
+        early, late = slice(0, EARLY), slice(EARLY, V)
+        early_reads = [sb("ra%d" % u, [P, PLANES, EARLY], F32) for u in range(2)]
+        early_sum = sb("oa", [P, PLANES, EARLY], F32)
+        late_sum = sb("ob", [P, PLANES, LATE], F32)
+        early_16 = sb("oa16", [P, EARLY, PLANES], BF16)
+        late_16 = sb("ob16", [P, LATE, PLANES], BF16)
         lists = (c1_t, c2_t)
 
-        def read(dst, u, t, cols):
-            nc.vector.tensor_tensor(dst[u][:, t, :], h[t][:].indirect(lists[u][:, cols.start // PER_COLUMN : cols.stop // PER_COLUMN]), g_t[u][:, cols], MULT)
+        def read(reads, u, t, cols):
+            nc.vector.tensor_tensor(reads[u][:, t, :], h[t][:].indirect(entries(lists[u], cols)), g_t[u][:, cols], MULT)
 
-        def add_a(t):
-            nc.vector.tensor_tensor(oa[:, t, :], ra[0][:, t, :], ra[1][:, t, :], ADD)
-            nc.sync.dma_start(out=out_rows[:, t, 0:VA], in_=oa[:, t, :])
+        def add(total, reads, planes):
+            nc.vector.tensor_tensor(total[:, planes, :], reads[0][:, planes, :], reads[1][:, planes, :], ADD)
 
-        blocks = [slice(b, b + P) for b in range(0, VA, P)]
-        staged = [keep.tile([P, VA], F32, name="staged%d" % t, tag="staged%d" % t, align_bytes=64) for t in range(2)]
+        def store_early(t):
+            nc.sync.dma_start(out=out_rows[:, t, early], in_=early_sum[:, t, :])
+
+        blocks = [slice(b, b + P) for b in range(0, EARLY, P)]
+        staged = [sb("staged%d" % t, [P, EARLY], F32) for t in range(TURNED_PLANES)]
 
         def add_turned(t):
-            turned = turns.tile([P, VA], F32, name="turned", tag="turn")
+            turned = turns.tile([P, EARLY], F32, name="turned", tag="turn")
             for cols in blocks:
                 for u in range(2):
-                    nc.tensor.matmul(turned[:, cols], ra[u][:, t, cols], ident[:], start=(u == 0), stop=(u == 1), is_transpose=True)
+                    nc.tensor.matmul(turned[:, cols], early_reads[u][:, t, cols], ident[:], start=(u == 0), stop=(u == 1), is_transpose=True)
             nc.scalar.copy(staged[t][:], turned[:])
 
         def turn_back(t):
-            back = turns.tile([P, VA], F32, name="back", tag="turn")
+            back = turns.tile([P, EARLY], F32, name="back", tag="turn")
             for cols in blocks:
                 nc.tensor.transpose(back[:, cols], staged[t][:, cols], ident[:])
-            nc.scalar.copy(oa[:, t, :], back[:])
-            nc.sync.dma_start(out=out_rows[:, t, 0:VA], in_=oa[:, t, :])
+            nc.scalar.copy(early_sum[:, t, :], back[:])
+            store_early(t)
 
-        def quant(src, cols):
-            nc.vector.quantize_mx(out=oc[:, cols].bitcast(FP8X4), scales=os_[:, cols], in_=src.rearrange("p n t -> p (n t)"))
+        for t in range(TURNED_PLANES):
+            read(early_reads, 0, t, early)
+            read(early_reads, 1, t, early)
+            add_turned(t)
+        for t in range(TURNED_PLANES):
+            turn_back(t)
 
-        ca, cb = slice(0, VA), slice(VA, V)
-        for t in range(PACK):
-            read(ra, 0, t, ca)
-            if t == 3:
-                add_a(2)
-            read(ra, 1, t, ca)
-            if t < 2:
-                add_turned(t)
-            if t == 1:
-                turn_back(0)
-                turn_back(1)
-        rb = [keep.tile([P, PACK, VB], F32, name="rb%d" % u, tag="staged%d" % u, align_bytes=64) for u in range(2)]
-        read(rb, 0, 0, cb)
-        add_a(3)
-        parts = (slice(0, 256), slice(256, VA))
-        for cols in parts:
-            nc.scalar.copy(oa16[:, cols, :], oa[:, :, cols].rearrange("p t n -> p n t"))
-        read(rb, 1, 0, cb)
+        read(early_reads, 0, 2, early)
+        read(early_reads, 1, 2, early)
+        read(early_reads, 0, 3, early)
+        add(early_sum, early_reads, 2)
+        store_early(2)
+        read(early_reads, 1, 3, early)
+        late_reads = [sb("rb%d" % u, [P, PLANES, LATE], F32, buffer="staged%d" % u) for u in range(2)]
+        read(late_reads, 0, 0, late)
+        add(early_sum, early_reads, 3)
+        store_early(3)
+
+        early_parts = (slice(0, 2 * P), slice(2 * P, EARLY))
+        for cols in early_parts:
+            nc.scalar.copy(early_16[:, cols, :], early_sum[:, :, cols].rearrange("p t n -> p n t"))
+        read(late_reads, 1, 0, late)
         for t in (1, 2):
-            read(rb, 0, t, cb)
-            read(rb, 1, t, cb)
-        read(rb, 0, 3, cb)
-        nc.vector.tensor_tensor(ob[:, 0:3, :], rb[0][:, 0:3, :], rb[1][:, 0:3, :], ADD)
-        read(rb, 1, 3, cb)
-        quant(oa16[:, parts[0], :], parts[0])
-        nc.vector.tensor_tensor(ob[:, 3, :], rb[0][:, 3, :], rb[1][:, 3, :], ADD)
-        nc.sync.dma_start(out=out_rows[:, :, cb], in_=ob[:])
-        quant(oa16[:, parts[1], :], parts[1])
-        nc.scalar.dma_start(out=words[:, ca], in_=oc[:, ca].bitcast(I32))
-        nc.vector.tensor_copy(ob16[:], ob[:].rearrange("p t n -> p n t"))
-        quant(ob16[:], cb)
-        nc.sync.dma_start(out=words[:, cb], in_=oc[:, cb].bitcast(I32))
-        for q in range(4):
-            queue = nc.scalar if q % 2 == 0 else nc.sync
-            queue.dma_start(out=out_2[0, 4 * q : 4 * q + 4, :].bitcast(I32), in_=os_[32 * q : 32 * q + 4, :].bitcast(I32))
+            read(late_reads, 0, t, late)
+            read(late_reads, 1, t, late)
+        read(late_reads, 0, 3, late)
+        add(late_sum, late_reads, slice(0, 3))
+        read(late_reads, 1, 3, late)
+
+        quantise(oc, osc, early_parts[0], early_16[:, early_parts[0], :])
+        add(late_sum, late_reads, 3)
+        nc.sync.dma_start(out=out_rows[:, :, late], in_=late_sum[:])
+        quantise(oc, osc, early_parts[1], early_16[:, early_parts[1], :])
+        nc.scalar.dma_start(out=out_words[:, early], in_=oc[:, early].bitcast(I32))
+        nc.vector.tensor_copy(late_16[:], late_sum[:].rearrange("p t n -> p n t"))
+        quantise(oc, osc, late, late_16[:])
+
+        nc.sync.dma_start(out=out_words[:, late], in_=oc[:, late].bitcast(I32))
+        for q in range(P // QUADRANT):
+            queue = (nc.scalar, nc.sync)[q % 2]
+            queue.dma_start(out=out_2[0, 4 * q : 4 * q + 4, :].bitcast(I32), in_=osc[QUADRANT * q : QUADRANT * q + 4, :].bitcast(I32))

from contextlib import ExitStack

import concourse.mybir as mybir
from concourse.masks import make_identity

K, T, S, V, N, U, H = 512, 2048, 512, 512, 512, 1024, 512
FLOPS = 2 * K * H * S + 2 * H * N * U

F32 = mybir.dt.float32
BF16 = mybir.dt.bfloat16
I32 = mybir.dt.int32
U32 = mybir.dt.uint32
U16 = mybir.dt.uint16
U8 = mybir.dt.uint8
FP8X4 = mybir.dt.float8_e4m3fn_x4
MULT = mybir.AluOpType.mult
ADD = mybir.AluOpType.add
RELU = mybir.ActivationFunctionType.Relu
COPY = mybir.ActivationFunctionType.Copy

P = 128
PLANES = 4
ENTRIES_PER_COLUMN = 16
QUADRANT = 32
SCALE_ROWS = 16
BANK = 512
PRODUCT_BANKS = 6
TURN_BANKS = 2

SCATTER_ORDER = (2, 0, 1, 3)
Z_CHUNK = 256
VECTOR_PLACES = 640
H0_PIECES = ((0, 256), (256, 512), (512, 768), (768, 896), (896, 1024))
EARLY = 384
LATE = V - EARLY
TURNED_PLANES = 2


def tile_picked_dcomb_relu_po_kernel(tc, x_words, x_scales, w1, w2_words, w2_scales, g1, g2, offs, slot, c1, c2, out_0, out_1, out_2):
    nc = tc.nc
    with ExitStack() as ctx:
        keep = ctx.enter_context(tc.tile_pool(name="keep", bufs=1))
        psum = ctx.enter_context(tc.psum_pool(name="psum", bufs=PRODUCT_BANKS))
        turns = ctx.enter_context(tc.psum_pool(name="turns", bufs=TURN_BANKS))

        def sb(name, shape, dtype, buffer=None):
            return keep.tile(shape, dtype, name=name, tag=buffer or name, align_bytes=64)

        def entries(offsets, cols):
            return offsets[:, cols.start // ENTRIES_PER_COLUMN : cols.stop // ENTRIES_PER_COLUMN]

        def as_words(packed):
            return packed[0].rearrange("p n t -> p (n t)").bitcast(I32)

        def load_scale_rows(tile, rows):
            for r in range(4):
                nc.sync.dma_start(out=tile[r:P:QUADRANT, :].bitcast(I32), in_=rows[r:SCALE_ROWS:4, :].bitcast(I32))

        def product(name, codes, scales, moving, moving_scales, cols):
            acc = psum.tile([P, cols.stop - cols.start], F32, name=name, tag="bank")
            nc.tensor.matmul_mx(
                out=acc[:],
                lhsT=codes.bitcast(FP8X4),
                lhsT_scale=scales,
                rhs=moving[:, cols].bitcast(FP8X4),
                rhs_scale=moving_scales[:, cols],
                start=True,
                stop=True,
            )
            return acc

        def quantise(codes, scales, cols, grouped):
            nc.vector.quantize_mx(out=codes[:, cols].bitcast(FP8X4), scales=scales[:, cols], in_=grouped.rearrange("p n t -> p (n t)"))

        offs_t = sb("offs_t", [P, S // ENTRIES_PER_COLUMN], U16)
        slot_t = sb("slot_t", [P, S // ENTRIES_PER_COLUMN], U16)
        c1_t = sb("c1_t", [P, V // ENTRIES_PER_COLUMN], U16)
        c2_t = sb("c2_t", [P, V // ENTRIES_PER_COLUMN], U16)
        xw = sb("xw", [P, T], U32)
        xs = sb("xs", [P, T], U8)
        w2w = sb("w2w", [P, N], U32)
        w2s = sb("w2s", [P, N], U8)
        w1_half = [sb("w1_half%d" % u, [P, PLANES, H // 2], F32) for u in range(2)]
        g_t = [sb("g%d" % u, [P, V], F32) for u in range(2)]
        d = [sb("d%d" % t, [P, U], F32) for t in range(PLANES)]

        nc.gpsimd.memset(xs[:].bitcast(I32), 0)
        w1_rows = w1.rearrange("(p j) c -> p j c", j=PLANES)
        nc.sync.dma_start(out=w1_half[0][:], in_=w1_rows[:, :, 0 : H // 2])
        nc.sync.dma_start(offs_t[:], offs)
        load_scale_rows(xs, x_scales[0])
        nc.sync.dma_start(out=w1_half[1][:], in_=w1_rows[:, :, H // 2 : H])
        nc.sync.dma_start(out=xw[:].bitcast(I32), in_=as_words(x_words))
        nc.sync.dma_start(slot_t[:], slot)
        nc.vector.memset(w2s[:].bitcast(I32), 0)
        nc.sync.dma_start(out=w2w[:].bitcast(I32), in_=as_words(w2_words))
        load_scale_rows(w2s, w2_scales[0])
        nc.sync.dma_start(c1_t[:], c1)
        nc.sync.dma_start(c2_t[:], c2)
        nc.sync.dma_start(out=g_t[0][:], in_=g1)
        nc.sync.dma_start(out=g_t[1][:], in_=g2)

        for t in SCATTER_ORDER[:2]:
            nc.vector.memset(d[t][:], 0.0)
        for t in SCATTER_ORDER[2:]:
            nc.gpsimd.memset(d[t][:], 0.0)

        ident = sb("ident", [P, P], F32)
        make_identity(nc, ident[:])

        xsg = sb("xsg", [P, S], U8)
        nc.vector.tensor_copy(xsg[:], xs[:].indirect(offs_t[:]))

        w1b = sb("w1b", [P, PLANES, P, PLANES], BF16)
        w1_dst = [w1b[:, :, u * P // 2 : (u + 1) * P // 2, :].rearrange("p t m j -> p m t j") for u in range(2)]
        w1_src = [w1_half[u][:].rearrange("p j (m t) -> p m t j", t=PLANES) for u in range(2)]
        nc.scalar.activation(w1_dst[0], w1_src[0], COPY)
        nc.vector.tensor_copy(w1_dst[1], w1_src[1])
        w1c = sb("w1c", [P, H], U32)
        w1s = sb("w1s", [P, H], U8)
        quantise(w1c, w1s, slice(0, H), w1b[:].rearrange("p t m j -> p (t m) j"))

        halves = (slice(0, S // 2), slice(S // 2, S))
        xg = sb("xg", [P, S], U32)
        for cols in halves:
            nc.vector.tensor_copy(xg[:, cols], xw[:].indirect(entries(offs_t, cols)))

        def y_product(t, cols):
            return product("y_acc", w1c[:, t * P : (t + 1) * P], w1s[:, t * P : (t + 1) * P], xg, xsg, cols)

        first, middle, last = SCATTER_ORDER[0], SCATTER_ORDER[1:-1], SCATTER_ORDER[-1]
        tokens = slice(0, S)
        y = {t: sb("y%d" % t, [P, S], F32) for t in middle}
        y[first] = sb("y_first", [P, S], F32, buffer="y_ends")
        for t, cols in [(first, half) for half in halves] + [(t, tokens) for t in middle]:
            acc = y_product(t, cols)
            nc.scalar.copy(y[t][:, cols], acc[:])
        last_acc = y_product(last, tokens)

        w2w_mt = w2w[:].rearrange("p (m t) -> p m t", t=PLANES)
        w2s_mt = w2s[:].rearrange("p (m t) -> p m t", t=PLANES)

        n_chunks = U // Z_CHUNK
        z = [sb("z%d" % c, [P, Z_CHUNK, PLANES], BF16) for c in range(n_chunks)]

        def scatter(t, cols):
            nc.vector.tensor_copy(d[t][:].indirect(entries(slot_t, cols)), y[t][:, cols])

        def relu_on_scalar(dst, src):
            nc.scalar.activation(dst, src, RELU)

        def relu_on_vector(dst, src):
            nc.vector.tensor_scalar_max(dst, src, 0.0)

        def round_plane(t, lo, hi, relu):
            for c in range(lo // Z_CHUNK, (hi - 1) // Z_CHUNK + 1):
                a, b = max(lo, c * Z_CHUNK), min(hi, (c + 1) * Z_CHUNK)
                relu(z[c][:, a - c * Z_CHUNK : b - c * Z_CHUNK, t], d[t][:, a:b])

        scatter(first, halves[0])
        w2w_0 = sb("w2w_0", [P, P], U32)
        nc.vector.tensor_copy(w2w_0[:], w2w_mt[:, :, 0])
        w2s_0 = sb("w2s_0", [P, P], U8)
        nc.vector.tensor_copy(w2s_0[:], w2s_mt[:, :, 0])
        scatter(first, halves[1])
        round_plane(first, 0, U, relu_on_scalar)
        y[last] = sb("y_last", [P, S], F32, buffer="y_ends")
        nc.scalar.copy(y[last][:], last_acc[:])
        for t in middle:
            scatter(t, tokens)
            round_plane(t, 0, U, relu_on_scalar)
        scatter(last, tokens)
        round_plane(last, VECTOR_PLACES, U, relu_on_scalar)
        round_plane(last, 0, VECTOR_PLACES, relu_on_vector)

        zc = sb("zc", [P, U], U32)
        zs = sb("zs", [P, U], U8)
        h = [sb("h%d" % t, [P, U], F32) for t in range(PLANES)]
        for lo, hi in H0_PIECES:
            c = lo // Z_CHUNK
            cols = slice(lo, hi)
            quantise(zc, zs, cols, z[c][:, lo - c * Z_CHUNK : hi - c * Z_CHUNK, :])
            acc = product("h_acc", w2w_0[:], w2s_0[:], zc, zs, cols)
            nc.scalar.copy(h[0][:, cols], acc[:])

        w2w_r = sb("w2w_r", [P, PLANES - 1, P], U32, buffer="z%d" % (n_chunks - 1))
        w2s_r = sb("w2s_r", [P, PLANES - 1, P], U8, buffer="z%d" % (n_chunks - 2))
        nc.vector.tensor_copy(w2w_r[:].rearrange("p t m -> p m t"), w2w_mt[:, :, 1:])
        nc.vector.tensor_copy(w2s_r[:].rearrange("p t m -> p m t"), w2s_mt[:, :, 1:])
        for t in range(1, PLANES):
            for lo in range(0, U, BANK):
                cols = slice(lo, lo + BANK)
                acc = product("h_acc", w2w_r[:, t - 1, :], w2s_r[:, t - 1, :], zc, zs, cols)
                nc.scalar.copy(h[t][:, cols], acc[:])

        out_rows = out_0.rearrange("(p t) v -> p t v", t=PLANES)
        oc = sb("oc", [P, V], U32)
        osc = sb("os", [P, V], U8)
        out_words = as_words(out_1)
        early, late = slice(0, EARLY), slice(EARLY, V)
        early_reads = [sb("ra%d" % u, [P, PLANES, EARLY], F32) for u in range(2)]
        early_sum = sb("oa", [P, PLANES, EARLY], F32)
        late_sum = sb("ob", [P, PLANES, LATE], F32)
        early_16 = sb("oa16", [P, EARLY, PLANES], BF16)
        late_16 = sb("ob16", [P, LATE, PLANES], BF16)
        lists = (c1_t, c2_t)

        def read(reads, u, t, cols):
            nc.vector.tensor_tensor(reads[u][:, t, :], h[t][:].indirect(entries(lists[u], cols)), g_t[u][:, cols], MULT)

        def add(total, reads, planes):
            nc.vector.tensor_tensor(total[:, planes, :], reads[0][:, planes, :], reads[1][:, planes, :], ADD)

        def store_early(t):
            nc.sync.dma_start(out=out_rows[:, t, early], in_=early_sum[:, t, :])

        blocks = [slice(b, b + P) for b in range(0, EARLY, P)]
        staged = [sb("staged%d" % t, [P, EARLY], F32) for t in range(TURNED_PLANES)]

        def add_turned(t):
            turned = turns.tile([P, EARLY], F32, name="turned", tag="turn")
            for cols in blocks:
                for u in range(2):
                    nc.tensor.matmul(turned[:, cols], early_reads[u][:, t, cols], ident[:], start=(u == 0), stop=(u == 1), is_transpose=True)
            nc.scalar.copy(staged[t][:], turned[:])

        def turn_back(t):
            back = turns.tile([P, EARLY], F32, name="back", tag="turn")
            for cols in blocks:
                nc.tensor.transpose(back[:, cols], staged[t][:, cols], ident[:])
            nc.scalar.copy(early_sum[:, t, :], back[:])
            store_early(t)

        for t in range(TURNED_PLANES):
            read(early_reads, 0, t, early)
            read(early_reads, 1, t, early)
            add_turned(t)
        for t in range(TURNED_PLANES):
            turn_back(t)

        read(early_reads, 0, 2, early)
        read(early_reads, 1, 2, early)
        read(early_reads, 0, 3, early)
        add(early_sum, early_reads, 2)
        store_early(2)
        read(early_reads, 1, 3, early)
        late_reads = [sb("rb%d" % u, [P, PLANES, LATE], F32, buffer="staged%d" % u) for u in range(2)]
        read(late_reads, 0, 0, late)
        add(early_sum, early_reads, 3)
        store_early(3)

        early_parts = (slice(0, 2 * P), slice(2 * P, EARLY))
        for cols in early_parts:
            nc.scalar.copy(early_16[:, cols, :], early_sum[:, :, cols].rearrange("p t n -> p n t"))
        read(late_reads, 1, 0, late)
        for t in (1, 2):
            read(late_reads, 0, t, late)
            read(late_reads, 1, t, late)
        read(late_reads, 0, 3, late)
        add(late_sum, late_reads, slice(0, 3))
        read(late_reads, 1, 3, late)

        quantise(oc, osc, early_parts[0], early_16[:, early_parts[0], :])
        add(late_sum, late_reads, 3)
        nc.sync.dma_start(out=out_rows[:, :, late], in_=late_sum[:])
        quantise(oc, osc, early_parts[1], early_16[:, early_parts[1], :])
        nc.scalar.dma_start(out=out_words[:, early], in_=oc[:, early].bitcast(I32))
        nc.vector.tensor_copy(late_16[:], late_sum[:].rearrange("p t n -> p n t"))
        quantise(oc, osc, late, late_16[:])

        nc.sync.dma_start(out=out_words[:, late], in_=oc[:, late].bitcast(I32))
        for q in range(P // QUADRANT):
            queue = (nc.scalar, nc.sync)[q % 2]
            queue.dma_start(out=out_2[0, 4 * q : 4 * q + 4, :].bitcast(I32), in_=osc[QUADRANT * q : QUADRANT * q + 4, :].bitcast(I32))
